import numpy as np
import ml_dtypes


def mxq(x, axis, fmt="e4m3"):
    dtype, down = {"e4m3": (ml_dtypes.float8_e4m3fn, 7), "e5m2": (ml_dtypes.float8_e5m2, 14)}[fmt]
    v = np.moveaxis(np.asarray(x, np.float32).astype(ml_dtypes.bfloat16).astype(np.float64), axis, -1)
    blocks = v.reshape(v.shape[:-1] + (-1, 32))
    amax = np.abs(blocks).max(-1, keepdims=True)
    byte = np.maximum(np.where(amax > 0, np.frexp(amax)[1] - 1 + 127, 0) - down, 1)
    scale = np.exp2(byte - 127.0)
    codes = (blocks / scale).astype(np.float32).astype(dtype).astype(np.float64)
    return np.moveaxis((codes * scale).reshape(v.shape), -1, axis)


WIDE = False


def mx_kscale(k):
    if not WIDE:
        return np.ones(k)
    levels = np.array([10, -10, 5, -5, 0])
    if k % 512:
        return np.exp2(np.random.permutation(np.resize(levels, k // 32))).repeat(32)
    a = np.empty((k // 512, 16))
    for p in range(k // 512):
        a[p, :8] = np.random.permutation(np.resize(levels, 8))
        for g in range(8):
            far = levels[np.abs(levels - a[p, g]) >= 10]
            a[p, g + 8] = far[np.random.randint(len(far))]
    return np.exp2(a.ravel()).repeat(32)


BF16 = ml_dtypes.bfloat16


def bf(x):
    return np.asarray(x, np.float32).astype(BF16)


def f64(x):
    return np.asarray(x).astype(np.float64)


E2M1 = np.array([0.0, 0.5, 1.0, 1.5, 2.0, 3.0, 4.0, 6.0, -0.0, -0.5, -1.0, -1.5, -2.0, -3.0, -4.0, -6.0])


def pack_weight(w, fmt):
    k, n = w.shape
    w = f64(bf(w)).reshape(k // 32, 32, n)
    amax = np.abs(w).max(1)
    if fmt == "e4m3":
        byte = np.frexp(amax)[1] - 1 + 127 - 7
    else:
        mant, ex = np.frexp(amax / 6.0)
        byte = np.where(mant > 0.5, ex, ex - 1) + 127
    byte = np.clip(np.where(amax > 0, byte, 1), 1, 254)
    scaled = (w * np.exp2(127.0 - byte)[:, None, :]).reshape(k, n).astype(np.float32)
    by_word = np.ascontiguousarray(scaled.reshape(k // 512, 128, 4, n).transpose(0, 1, 3, 2))
    if fmt == "e4m3":
        words = by_word.astype(ml_dtypes.float8_e4m3fn).view(np.uint8)
    else:
        c = by_word.astype(ml_dtypes.float4_e2m1fn).view(np.uint8) & 0xF
        words = c[..., 0::2] | (c[..., 1::2] << 4)
    return np.ascontiguousarray(words), np.ascontiguousarray(byte.astype(np.uint8).reshape(k // 512, 16, n))


def unpack_weight(words, scales, fmt):
    g, p, n, _ = words.shape
    if fmt == "e4m3":
        vals = np.ascontiguousarray(words).view(ml_dtypes.float8_e4m3fn).astype(np.float64)
    else:
        nib = np.empty((g, p, n, 4), np.uint8)
        nib[..., 0::2] = words & 0xF
        nib[..., 1::2] = words >> 4
        vals = E2M1[nib]
    vals = vals * np.repeat(np.exp2(scales.astype(np.float64) - 127.0), 8, axis=1)[..., None]
    return vals.transpose(0, 1, 3, 2).reshape(g * 512, n)
def pack4(w):
    words, scales = pack_weight(w, "e2m1")
    return words.reshape(words.shape[0], 128, -1), scales


def unpack4(words, scales):
    return unpack_weight(words.reshape(words.shape[0], 128, -1, 2), scales, "e2m1")


B, I1, I2, R, J, N = 32, 128, 512, 8, 128, 512


def sigmoid(v):
    return 1.0 / (1.0 + np.exp(-v))


def setup_inputs():
    s = mx_kscale(I2)
    t = mx_kscale(R * I1)
    x = np.random.standard_normal((B, I1, I2)) * s
    a = np.random.standard_normal((I2, R * J)) / np.sqrt(I2) / s[:, None]
    c = np.random.standard_normal((R * I1, N)) / np.sqrt(R * I1) / t[:, None]
    a_words, a_scales = pack4(a)
    c_words, c_scales = pack4(c)
    return {"x": bf(x),
            "a_words": a_words, "a_scales": a_scales,
            "gate": bf(np.random.standard_normal((B, R))),
            "gain": bf((1.0 + 0.1 * np.random.standard_normal((R, I1))) * t.reshape(R, I1)),
            "c_words": c_words, "c_scales": c_scales,
            "bias": bf(0.3 * np.random.standard_normal((J, N)))}


def reference(x, a_words, a_scales, gate, gain, c_words, c_scales, bias):
    xq = mxq(f64(x).reshape(B * I1, I2), 1, "e4m3")
    y = xq @ unpack4(a_words, a_scales)
    y = y.reshape(B, I1, R, J).transpose(0, 3, 2, 1)
    h = y * sigmoid(f64(gate))[:, None, :, None] * f64(gain)[None, None, :, :]
    hq = mxq(h.reshape(B * J, R * I1), 1, "e4m3")
    z = hq @ unpack4(c_words, c_scales)
    return z.reshape(B, J, N) + f64(bias)[None, :, :]

@@ -1,0 +1,261 @@
+from contextlib import ExitStack
+
+import concourse.mybir as mybir
+from concourse.masks import make_identity
+
+B, I1, I2, R, J, N = 32, 128, 512, 8, 128, 512
+FLOPS = 2 * B * I1 * I2 * R * J + 2 * B * J * R * I1 * N
+
+F32 = mybir.dt.float32
+BF16 = mybir.dt.bfloat16
+I32 = mybir.dt.int32
+U32 = mybir.dt.uint32
+U8 = mybir.dt.uint8
+FP8X4 = mybir.dt.float8_e4m3fn_x4
+FP4X4 = mybir.dt.float4_e2m1fn_x4
+MULT = mybir.AluOpType.mult
+ADD = mybir.AluOpType.add
+
+P = 128
+GROUP = 4
+PAIRS = B // 2
+STEPS = 2 * B // GROUP
+X_AHEAD = 3
+OUT_LAG = 4
+
+
+def tile_gated_tensor_train_linear_f1_kernel(
+    tc, x, a_words, a_scales, gate, gain, c_words, c_scales, bias, out
+):
+    nc = tc.nc
+    with ExitStack() as ctx:
+        keep = ctx.enter_context(tc.tile_pool(name="keep", bufs=1))
+        work = ctx.enter_context(tc.tile_pool(name="work", bufs=3))
+        psum = ctx.enter_context(tc.psum_pool(name="psum", bufs=1))
+        ctx.enter_context(tc.manual_schedule())
+
+        def bank(tag):
+            return psum.tile([P, 512], F32, name=tag, tag=tag)
+
+        a_plane = keep.tile([P, R * J], U8, align_bytes=64)
+        c_plane = keep.tile([P, 2, N], U8, align_bytes=64)
+        rows = keep.tile([P, 256], BF16)
+        nc.vector.memset(rows[:].bitcast(I32), 0)
+        nc.vector.memset(a_plane[:].bitcast(I32), 0)
+        nc.vector.memset(c_plane[:].rearrange("p g n -> p (g n)").bitcast(I32), 0)
+        ident = keep.tile([P, P], F32)
+        make_identity(nc, ident[:])
+
+        x_sb = []
+
+        def load_x(pair):
+            t = keep.tile([P, 2, I2], BF16, name="x%d" % pair)
+            nc.sync.dma_start(out=t[:], in_=x[2 * pair : 2 * pair + 2].rearrange("b i c -> i b c"))
+            x_sb.append(t)
+
+        a_codes = keep.tile([P, 2 * R * J], U8, align_bytes=64)
+        c_codes = keep.tile([P, 2, 2 * N], U8, align_bytes=64)
+        bias_sb = keep.tile([P, N], BF16)
+
+        load_x(0)
+        nc.sync.dma_start(out=rows[0:R, 0:I1], in_=gain)
+        nc.sync.dma_start(out=rows[R : R + 1, :], in_=gate.rearrange("(o b) r -> o (b r)", o=1))
+        load_x(1)
+        nc.sync.dma_start(out=a_codes[:].bitcast(I32), in_=a_words[0].bitcast(I32))
+        for q in range(4):
+            nc.sync.dma_start(
+                out=a_plane[32 * q : 32 * q + 4, :].bitcast(I32),
+                in_=a_scales[0, 4 * q : 4 * q + 4, :].bitcast(I32),
+            )
+        load_x(2)
+        load_x(3)
+        load_x(4)
+        nc.sync.dma_start(out=c_codes[:].bitcast(I32), in_=c_words.rearrange("g p n -> p g n").bitcast(I32))
+        for q in range(4):
+            nc.sync.dma_start(
+                out=c_plane[32 * q : 32 * q + 4, :, :].bitcast(I32),
+                in_=c_scales[:, 4 * q : 4 * q + 4, :].rearrange("g s n -> s g n").bitcast(I32),
+            )
+        nc.sync.dma_start(out=bias_sb[:], in_=bias)
+        for pair in range(5, PAIRS):
+            load_x(pair)
+
+        pick = keep.tile([P, 16], BF16)
+        nc.vector.tensor_copy(out=pick[:], in_=ident[:, 0:16])
+        sig = keep.tile([P, B * R], F32)
+        gain_sb = keep.tile([P, R, I1], BF16)
+        spread = bank("y2")
+        nc.tensor.matmul(
+            spread[:, 0 : B * R], lhsT=pick[:, R : R + 1].to_broadcast([P, P]), rhs=rows[:], start=True, stop=True
+        )
+        nc.scalar.activation(out=sig[:], in_=spread[:, 0 : B * R], func=mybir.ActivationFunctionType.Sigmoid)
+        for half in range(2):
+            spread = bank("y%d" % half)
+            for rl in range(4):
+                r = 4 * half + rl
+                nc.tensor.matmul(
+                    spread[:, rl * I1 : (rl + 1) * I1],
+                    lhsT=pick[:, r : r + 1].to_broadcast([P, P]),
+                    rhs=rows[:, 0:I1],
+                    start=True,
+                    stop=True,
+                )
+            nc.vector.tensor_copy(
+                out=gain_sb[:, 4 * half : 4 * half + 4, :].rearrange("p r (u q e) -> p r u q e", u=2, e=2),
+                in_=spread[:].rearrange("p (r q u e) -> p r u q e", r=4, u=2, e=2),
+            )
+
+        x_grouped, x_codes, x_planes = {}, {}, {}
+        h_rows, h_grouped, h_codes, h_planes = {}, {}, {}, {}
+
+        def turn_x(pair):
+            xt = bank("xt" if pair % 2 or pair > X_AHEAD else "ht0")
+            for s in range(2):
+                words = x_sb[pair][:, s, :].bitcast(F32)
+                for w in range(2):
+                    col = (2 * s + w) * P
+                    nc.tensor.transpose(xt[:, col : col + P], words[:, w : 2 * P : 2], ident[:])
+            grouped = work.tile([P, 2 * I1 * 4], BF16, name="x_grouped", align_bytes=64)
+            for s in range(2):
+                nc.scalar.copy(
+                    out=grouped[:, s * 512 : (s + 1) * 512]
+                    .bitcast(F32)
+                    .rearrange("p (u q e w) -> p u q e w", u=2, e=2, w=2),
+                    in_=xt[:, s * 256 : (s + 1) * 256].rearrange("p (w q u e) -> p u q e w", w=2, u=2, e=2),
+                )
+            x_grouped[pair] = grouped
+
+        def quantize_x(pair):
+            group, half = divmod(pair, 2)
+            if half == 0:
+                x_codes[group] = work.tile([P, GROUP * I1], U32, name="x_codes", align_bytes=64)
+                x_planes[group] = work.tile([P, GROUP * I1], U8, name="x_plane", align_bytes=64)
+            cols = slice(half * 256, (half + 1) * 256)
+            nc.vector.quantize_mx(
+                out=x_codes[group][:, cols].bitcast(FP8X4), scales=x_planes[group][:, cols], in_=x_grouped[pair][:]
+            )
+
+        def first_matmul(step, rl, tag):
+            group, g = divmod(step, 2)
+            r = 4 * g + rl
+            y = bank(tag)
+            nc.tensor.matmul_mx(
+                out=y[:],
+                lhsT=a_codes[:, 2 * J * r : 2 * J * (r + 1)].bitcast(FP4X4),
+                lhsT_scale=a_plane[:, J * r : J * (r + 1)],
+                rhs=x_codes[group][:].bitcast(FP8X4),
+                rhs_scale=x_planes[group][:],
+                start=True,
+                stop=True,
+            )
+            return y
+
+        def weigh(step, rl, s, y):
+            group, g = divmod(step, 2)
+            r = 4 * g + rl
+            col = (GROUP * group + s) * R + r
+            nc.vector.scalar_tensor_tensor(
+                out=h_rows[step][:, s, :, 64 * rl : 64 * (rl + 1)],
+                in0=y[:, s * I1 : (s + 1) * I1].rearrange("p (u m) -> p u m", u=2),
+                scalar=sig[:, col : col + 1],
+                in1=gain_sb[:, r, :].rearrange("p (u m) -> p u m", u=2),
+                op0=MULT,
+                op1=MULT,
+            )
+
+        def turn_h(step, half):
+            if half == 0:
+                h_grouped[step] = work.tile([P, GROUP * J * 4], BF16, name="h_grouped", align_bytes=64)
+            ht = bank("ht%d" % half)
+            for s in range(2):
+                for u in range(2):
+                    col = (2 * s + u) * P
+                    nc.tensor.transpose(
+                        ht[:, col : col + P], h_rows[step][:, 2 * half + s, u, :].bitcast(F32), ident[:]
+                    )
+            nc.scalar.copy(
+                out=h_grouped[step][:, half * 1024 : (half + 1) * 1024]
+                .bitcast(F32)
+                .rearrange("p (s j u) -> p s j u", s=2, u=2),
+                in_=ht[:].rearrange("p (s u j) -> p s j u", s=2, u=2),
+            )
+
+        def quantize_h(step, first, count):
+            if first == 0:
+                h_codes[step] = work.tile([P, GROUP * J], U32, name="h_codes", bufs=6, align_bytes=64)
+                h_planes[step] = work.tile([P, GROUP * J], U8, name="h_plane", bufs=6, align_bytes=64)
+            cols = slice(first * J, (first + count) * J)
+            nc.vector.quantize_mx(
+                out=h_codes[step][:, cols].bitcast(FP8X4),
+                scales=h_planes[step][:, cols],
+                in_=h_grouped[step][:, 4 * first * J : 4 * (first + count) * J],
+            )
+
+        def second_matmul(b, direct):
+            group, s = divmod(b, GROUP)
+            z = bank("z%d" % (b % 2))
+            for g in range(2):
+                step = 2 * group + g
+                nc.tensor.matmul_mx(
+                    out=z[:],
+                    lhsT=h_codes[step][:, s * J : (s + 1) * J].bitcast(FP8X4),
+                    lhsT_scale=h_planes[step][:, s * J : (s + 1) * J],
+                    rhs=c_codes[:, g, :].bitcast(FP4X4),
+                    rhs_scale=c_plane[:, g, :],
+                    start=(g == 0),
+                    stop=(g == 1),
+                )
+            result = work.tile([P, N], F32, name="result", bufs=6)
+            if direct:
+                nc.vector.tensor_tensor(out=result[:], in0=z[:], in1=bias_sb[:], op=ADD)
+            else:
+                nc.scalar.copy(out=result[:], in_=z[:])
+                nc.gpsimd.tensor_tensor(out=result[:], in0=result[:], in1=bias_sb[:], op=ADD)
+            nc.sync.dma_start(out=out[b], in_=result[:])
+
+        for pair in range(2):
+            turn_x(pair)
+            quantize_x(pair)
+
+        y_turn = 0
+        for step in range(STEPS - 1):
+            h_rows[step] = work.tile([P, GROUP, 2, 256], BF16, name="h_rows")
+            pair_out = step - OUT_LAG
+            for rl in range(4):
+                if pair_out >= 0 and rl in (0, 3):
+                    second_matmul(2 * pair_out + rl // 3, False)
+                y = first_matmul(step, rl, "y%d" % (y_turn % 3))
+                y_turn = y_turn + 1
+                for s in range(GROUP):
+                    weigh(step, rl, s, y)
+            if step == 0:
+                turn_x(2)
+            else:
+                turn_h(step - 1, 0)
+                turn_h(step - 1, 1)
+            if step + X_AHEAD < PAIRS:
+                turn_x(step + X_AHEAD)
+            if step + 2 < PAIRS:
+                quantize_x(step + 2)
+            if step > 0:
+                quantize_h(step - 1, 0, GROUP)
+
+        last = STEPS - 1
+        h_rows[last] = work.tile([P, GROUP, 2, 256], BF16, name="h_rows")
+        ys = []
+        for rl in range(4):
+            ys.append(first_matmul(last, rl, "y%d" % ((y_turn + rl) % 3) if rl < 3 else "xt"))
+        for s in range(GROUP):
+            for rl in range(4):
+                weigh(last, rl, s, ys[rl])
+        turn_h(last - 1, 0)
+        turn_h(last - 1, 1)
+        quantize_h(last - 1, 0, GROUP)
+        pair_out = last - OUT_LAG
+        for half in range(2):
+            for s in range(2):
+                second_matmul(2 * (pair_out + half) + s, False)
+            turn_h(last, half)
+            quantize_h(last, 2 * half, 2)
+        for b in range(2 * (pair_out + 2), B):
+            second_matmul(b, b >= B - GROUP)

@@ -21,7 +21,20 @@ GROUP = 4
 PAIRS = B // 2
 STEPS = 2 * B // GROUP
 X_AHEAD = 3
+XOFF = 1
 OUT_LAG = 4
+ORDER = "aA0bB12QgpDqrHX3s"
+EORDER = "01QpqH23rsX"
+G_COLS = 1024
+Y_BANKS = 3
+Z_BANKS = 2
+TAIL_DIRECT = 4
+SORT = 0
+EARLY = 4
+WARM = 3
+TAIL = "Ww0HgQw1aAbBKq"
+GB = 8
+XDONE = 10
 
 
 def tile_gated_tensor_train_linear_f1_kernel(
@@ -40,6 +53,8 @@ def tile_gated_tensor_train_linear_f1_kernel(
         a_plane = keep.tile([P, R * J], U8, align_bytes=64)
         c_plane = keep.tile([P, 2, N], U8, align_bytes=64)
         rows = keep.tile([P, 256], BF16)
+        zeros = keep.tile([P, 512], BF16)
+        nc.vector.memset(zeros[:].bitcast(I32), 0)
         nc.vector.memset(rows[:].bitcast(I32), 0)
         nc.vector.memset(a_plane[:].bitcast(I32), 0)
         nc.vector.memset(c_plane[:].rearrange("p g n -> p (g n)").bitcast(I32), 0)
@@ -55,7 +70,7 @@ def tile_gated_tensor_train_linear_f1_kernel(
 
         a_codes = keep.tile([P, 2 * R * J], U8, align_bytes=64)
         c_codes = keep.tile([P, 2, 2 * N], U8, align_bytes=64)
-        bias_sb = keep.tile([P, N], BF16)
+        bias_sb = keep.tile([P, 2, N], BF16)
 
         load_x(0)
         nc.sync.dma_start(out=rows[0:R, 0:I1], in_=gain)
@@ -76,75 +91,70 @@ def tile_gated_tensor_train_linear_f1_kernel(
                 out=c_plane[32 * q : 32 * q + 4, :, :].bitcast(I32),
                 in_=c_scales[:, 4 * q : 4 * q + 4, :].rearrange("g s n -> s g n").bitcast(I32),
             )
-        nc.sync.dma_start(out=bias_sb[:], in_=bias)
+        for s in range(2):
+            nc.sync.dma_start(out=bias_sb[:, s, :], in_=bias)
         for pair in range(5, PAIRS):
             load_x(pair)
 
-        pick = keep.tile([P, 16], BF16)
-        nc.vector.tensor_copy(out=pick[:], in_=ident[:, 0:16])
-        sig = keep.tile([P, B * R], F32)
-        gain_sb = keep.tile([P, R, I1], BF16)
-        spread = bank("y2")
-        nc.tensor.matmul(
-            spread[:, 0 : B * R], lhsT=pick[:, R : R + 1].to_broadcast([P, P]), rhs=rows[:], start=True, stop=True
-        )
-        nc.scalar.activation(out=sig[:], in_=spread[:, 0 : B * R], func=mybir.ActivationFunctionType.Sigmoid)
-        for half in range(2):
-            spread = bank("y%d" % half)
-            for rl in range(4):
-                r = 4 * half + rl
-                nc.tensor.matmul(
-                    spread[:, rl * I1 : (rl + 1) * I1],
-                    lhsT=pick[:, r : r + 1].to_broadcast([P, P]),
-                    rhs=rows[:, 0:I1],
-                    start=True,
-                    stop=True,
-                )
-            nc.vector.tensor_copy(
-                out=gain_sb[:, 4 * half : 4 * half + 4, :].rearrange("p r (u q e) -> p r u q e", u=2, e=2),
-                in_=spread[:].rearrange("p (r q u e) -> p r u q e", r=4, u=2, e=2),
-            )
+        grouped, codes, planes, h_rows = {}, {}, {}, {}
 
-        x_grouped, x_codes, x_planes = {}, {}, {}
-        h_rows, h_grouped, h_codes, h_planes = {}, {}, {}, {}
+        def batch_width(batch):
+            group = (batch + XOFF) // 2
+            return (2048 if batch >= 2 else 0) + (2048 if (batch + XOFF) % 2 == 0 and 0 < group < B // GROUP else 0)
 
-        def turn_x(pair):
-            xt = bank("xt" if pair % 2 or pair > X_AHEAD else "ht0")
+        def staged(batch):
+            if batch not in grouped:
+                grouped[batch] = work.tile([P, 4096], BF16, name="grouped", tag="stage%d" % (batch % GB), bufs=1, align_bytes=64)
+            return grouped[batch]
+
+        def x_place(group):
+            batch = 2 * group - XOFF
+            return batch, (512 if batch >= 2 else 0)
+
+        def turn_x(pair, tag):
+            xt = bank(tag)
+            if SORT:
+                srt = work.tile([P, 2, 2, P], U32, name="x_sorted")
+                nc.scalar.copy(out=srt[:], in_=x_sb[pair][:].bitcast(U32).rearrange("p s (m w) -> p s w m", w=2))
             for s in range(2):
                 words = x_sb[pair][:, s, :].bitcast(F32)
                 for w in range(2):
                     col = (2 * s + w) * P
-                    nc.tensor.transpose(xt[:, col : col + P], words[:, w : 2 * P : 2], ident[:])
-            grouped = work.tile([P, 2 * I1 * 4], BF16, name="x_grouped", align_bytes=64)
+                    if SORT:
+                        nc.tensor.transpose(xt[:, col : col + P], srt[:, s, w, :].bitcast(F32), ident[:])
+                    else:
+                        nc.tensor.transpose(xt[:, col : col + P], words[:, w : 2 * P : 2], ident[:])
+            batch, first = x_place(pair // 2)
             for s in range(2):
+                col = 4 * (first + (2 * (pair % 2) + s) * I1)
                 nc.scalar.copy(
-                    out=grouped[:, s * 512 : (s + 1) * 512]
+                    out=staged(batch)[:, col : col + 512]
                     .bitcast(F32)
                     .rearrange("p (u q e w) -> p u q e w", u=2, e=2, w=2),
                     in_=xt[:, s * 256 : (s + 1) * 256].rearrange("p (w q u e) -> p u q e w", w=2, u=2, e=2),
                 )
-            x_grouped[pair] = grouped
 
-        def quantize_x(pair):
-            group, half = divmod(pair, 2)
-            if half == 0:
-                x_codes[group] = work.tile([P, GROUP * I1], U32, name="x_codes", align_bytes=64)
-                x_planes[group] = work.tile([P, GROUP * I1], U8, name="x_plane", align_bytes=64)
-            cols = slice(half * 256, (half + 1) * 256)
+        def quantize(batch, first, count):
+            if batch not in codes:
+                codes[batch] = work.tile([P, 1024], U32, name="codes", bufs=7, align_bytes=64)
+                planes[batch] = work.tile([P, 1024], U8, name="plane", bufs=7, align_bytes=64)
             nc.vector.quantize_mx(
-                out=x_codes[group][:, cols].bitcast(FP8X4), scales=x_planes[group][:, cols], in_=x_grouped[pair][:]
+                out=codes[batch][:, first : first + count].bitcast(FP8X4),
+                scales=planes[batch][:, first : first + count],
+                in_=grouped[batch][:, 4 * first : 4 * (first + count)],
             )
 
         def first_matmul(step, rl, tag):
             group, g = divmod(step, 2)
             r = 4 * g + rl
+            batch, first = x_place(group)
             y = bank(tag)
             nc.tensor.matmul_mx(
                 out=y[:],
                 lhsT=a_codes[:, 2 * J * r : 2 * J * (r + 1)].bitcast(FP4X4),
                 lhsT_scale=a_plane[:, J * r : J * (r + 1)],
-                rhs=x_codes[group][:].bitcast(FP8X4),
-                rhs_scale=x_planes[group][:],
+                rhs=codes[batch][:, first : first + 512].bitcast(FP8X4),
+                rhs_scale=planes[batch][:, first : first + 512],
                 start=True,
                 stop=True,
             )
@@ -155,7 +165,7 @@ def tile_gated_tensor_train_linear_f1_kernel(
             r = 4 * g + rl
             col = (GROUP * group + s) * R + r
             nc.vector.scalar_tensor_tensor(
-                out=h_rows[step][:, s, :, 64 * rl : 64 * (rl + 1)],
+                out=h_rows[step, s // 2][:, s % 2, :, 64 * rl : 64 * (rl + 1)],
                 in0=y[:, s * I1 : (s + 1) * I1].rearrange("p (u m) -> p u m", u=2),
                 scalar=sig[:, col : col + 1],
                 in1=gain_sb[:, r, :].rearrange("p (u m) -> p u m", u=2),
@@ -164,98 +174,182 @@ def tile_gated_tensor_train_linear_f1_kernel(
             )
 
         def turn_h(step, half):
-            if half == 0:
-                h_grouped[step] = work.tile([P, GROUP * J * 4], BF16, name="h_grouped", align_bytes=64)
             ht = bank("ht%d" % half)
             for s in range(2):
                 for u in range(2):
                     col = (2 * s + u) * P
                     nc.tensor.transpose(
-                        ht[:, col : col + P], h_rows[step][:, 2 * half + s, u, :].bitcast(F32), ident[:]
+                        ht[:, col : col + P], h_rows[step, half][:, s, u, :].bitcast(F32), ident[:]
                     )
             nc.scalar.copy(
-                out=h_grouped[step][:, half * 1024 : (half + 1) * 1024]
+                out=staged(step + 2)[:, half * 1024 : (half + 1) * 1024]
                 .bitcast(F32)
                 .rearrange("p (s j u) -> p s j u", s=2, u=2),
                 in_=ht[:].rearrange("p (s u j) -> p s j u", s=2, u=2),
             )
 
-        def quantize_h(step, first, count):
-            if first == 0:
-                h_codes[step] = work.tile([P, GROUP * J], U32, name="h_codes", bufs=6, align_bytes=64)
-                h_planes[step] = work.tile([P, GROUP * J], U8, name="h_plane", bufs=6, align_bytes=64)
-            cols = slice(first * J, (first + count) * J)
-            nc.vector.quantize_mx(
-                out=h_codes[step][:, cols].bitcast(FP8X4),
-                scales=h_planes[step][:, cols],
-                in_=h_grouped[step][:, 4 * first * J : 4 * (first + count) * J],
-            )
+        results, summed, zs = {}, {}, {}
 
-        def second_matmul(b, direct):
+        def second_matmul(b, tag):
             group, s = divmod(b, GROUP)
-            z = bank("z%d" % (b % 2))
+            z = bank(tag)
             for g in range(2):
-                step = 2 * group + g
+                batch = 2 * group + g + 2
                 nc.tensor.matmul_mx(
                     out=z[:],
-                    lhsT=h_codes[step][:, s * J : (s + 1) * J].bitcast(FP8X4),
-                    lhsT_scale=h_planes[step][:, s * J : (s + 1) * J],
+                    lhsT=codes[batch][:, s * J : (s + 1) * J].bitcast(FP8X4),
+                    lhsT_scale=planes[batch][:, s * J : (s + 1) * J],
                     rhs=c_codes[:, g, :].bitcast(FP4X4),
                     rhs_scale=c_plane[:, g, :],
                     start=(g == 0),
                     stop=(g == 1),
                 )
-            result = work.tile([P, N], F32, name="result", bufs=6)
-            if direct:
-                nc.vector.tensor_tensor(out=result[:], in0=z[:], in1=bias_sb[:], op=ADD)
-            else:
-                nc.scalar.copy(out=result[:], in_=z[:])
-                nc.gpsimd.tensor_tensor(out=result[:], in0=result[:], in1=bias_sb[:], op=ADD)
-            nc.sync.dma_start(out=out[b], in_=result[:])
+            zs[b] = z
+            if b % 2 == 0:
+                results[b // 2] = work.tile([P, 2 * N], F32, name="result", bufs=4)
 
-        for pair in range(2):
-            turn_x(pair)
-            quantize_x(pair)
+        def copy_out(b):
+            base = (b % 2) * N
+            nc.scalar.copy(out=results[b // 2][:, base : base + N], in_=zs[b][:])
 
-        y_turn = 0
-        for step in range(STEPS - 1):
-            h_rows[step] = work.tile([P, GROUP, 2, 256], BF16, name="h_rows")
-            pair_out = step - OUT_LAG
+        def add_direct(b):
+            base = (b % 2) * N
+            summed[b // 2] = results[b // 2]
+            nc.vector.tensor_tensor(out=results[b // 2][:, base : base + N], in0=zs[b][:], in1=bias_sb[:, 0, :], op=ADD)
+
+        def add_copied(pair, first, count):
+            nc.gpsimd.tensor_tensor(
+                out=summed[pair][:, first : first + count],
+                in0=results[pair][:, first : first + count],
+                in1=bias_sb[:].rearrange("p s n -> p (s n)")[:, first : first + count],
+                op=ADD,
+            )
+
+        def store(first, count):
+            base = (first % 2) * N
+            nc.sync.dma_start(
+                out=out[first : first + count].rearrange("b j n -> j b n"),
+                in_=summed[first // 2][:, base : base + count * N].rearrange("p (s n) -> p s n", s=count),
+            )
+
+        warm = bank("y0")
+        for k in range(WARM):
+            nc.tensor.matmul(warm[:], lhsT=zeros[:, 0:P], rhs=zeros[:], start=True, stop=True)
+        turn_x(0, "ht0")
+        turn_x(1, "ht1")
+        pick = keep.tile([P, 16], BF16)
+        nc.vector.tensor_copy(out=pick[:], in_=ident[:, 0:16])
+        quantize(-XOFF, 0, 256)
+        quantize(-XOFF, 256, 256)
+        sig = keep.tile([P, B * R], F32)
+        gain_sb = keep.tile([P, R, I1], BF16)
+        spread = bank("xt")
+        nc.tensor.matmul(
+            spread[:, 0 : B * R], lhsT=pick[:, R : R + 1].to_broadcast([P, P]), rhs=rows[:], start=True, stop=True
+        )
+        nc.scalar.activation(out=sig[:], in_=spread[:, 0 : B * R], func=mybir.ActivationFunctionType.Sigmoid)
+        for half in range(2):
+            spread = bank(["y2", "z1"][half])
             for rl in range(4):
-                if pair_out >= 0 and rl in (0, 3):
-                    second_matmul(2 * pair_out + rl // 3, False)
-                y = first_matmul(step, rl, "y%d" % (y_turn % 3))
-                y_turn = y_turn + 1
-                for s in range(GROUP):
-                    weigh(step, rl, s, y)
-            if step == 0:
-                turn_x(2)
-            else:
-                turn_h(step - 1, 0)
-                turn_h(step - 1, 1)
-            if step + X_AHEAD < PAIRS:
-                turn_x(step + X_AHEAD)
-            if step + 2 < PAIRS:
-                quantize_x(step + 2)
-            if step > 0:
-                quantize_h(step - 1, 0, GROUP)
+                r = 4 * half + rl
+                nc.tensor.matmul(
+                    spread[:, rl * I1 : (rl + 1) * I1],
+                    lhsT=pick[:, r : r + 1].to_broadcast([P, P]),
+                    rhs=rows[:, 0:I1],
+                    start=True,
+                    stop=True,
+                )
+            copy = nc.scalar.copy if half else nc.vector.tensor_copy
+            copy(
+                out=gain_sb[:, 4 * half : 4 * half + 4, :].rearrange("p r (u q e) -> p r u q e", u=2, e=2),
+                in_=spread[:].rearrange("p (r q u e) -> p r u q e", r=4, u=2, e=2),
+            )
 
+        def sum_over(pair, batch):
+            summed[pair] = work.tile(
+                [P, 2 * N], F32, name="summed", tag="stage%d" % (batch % GB), bufs=1, align_bytes=64
+            )
+
+        def second_stage(pair):
+            for b in (2 * pair, 2 * pair + 1):
+                second_matmul(b, "z%d" % (b % 2))
+                copy_out(b)
+
+        def weigh_rank(step, rl, y):
+            for s in range(GROUP):
+                weigh(step, rl, s, y)
+
+        next_x = 2
+        y_turn = 0
         last = STEPS - 1
-        h_rows[last] = work.tile([P, GROUP, 2, 256], BF16, name="h_rows")
-        ys = []
-        for rl in range(4):
-            ys.append(first_matmul(last, rl, "y%d" % ((y_turn + rl) % 3) if rl < 3 else "xt"))
+        for step in range(STEPS):
+            for half in range(2):
+                h_rows[step, half] = work.tile([P, 2, 2, 256], BF16, name="h_rows", bufs=6)
+            pair_out = step - OUT_LAG
+            if pair_out < 0:
+                y_tags = ["z0", "y0", "y1", "y2"]
+                ys = [first_matmul(step, rl, y_tags[rl]) for rl in range(2)]
+                if step > 0:
+                    quantize(step, 0, batch_width(step) // 4)
+                    turn_h(step - 1, 0)
+                    turn_h(step - 1, 1)
+                else:
+                    turn_x(next_x, "ht0")
+                    turn_x(next_x + 1, "ht1")
+                    next_x = next_x + 2
+                ys.extend([first_matmul(step, rl, y_tags[rl]) for rl in range(2, 4)])
+                for rl in range(4):
+                    weigh_rank(step, rl, ys[rl])
+                if step > 0:
+                    turn_x(next_x, "xt")
+                    turn_x(next_x + 1, "z1")
+                    next_x = next_x + 2
+                continue
+            second_stage(pair_out)
+            x_left = next_x < PAIRS
+            if x_left or step == XDONE:
+                y_tags = ["y%d" % ((y_turn + rl) % 3) for rl in range(4)]
+                y_turn = y_turn + 4
+                if not x_left:
+                    y_tags[3] = "xt"
+            ys = [first_matmul(step, rl, y_tags[rl]) for rl in range(3 if x_left else 4)]
+            quantize(step, 0, batch_width(step) // 4)
+            sum_over(pair_out, step)
+            add_copied(pair_out, 0, 2 * N)
+            store(2 * pair_out, 2)
+            if step == last:
+                break
+            for rl in range(3):
+                weigh_rank(step, rl, ys[rl])
+            turn_h(step - 1, 0)
+            turn_h(step - 1, 1)
+            if x_left:
+                turn_x(next_x, "xt")
+                next_x = next_x + 1
+                ys.append(first_matmul(step, 3, y_tags[3]))
+            weigh_rank(step, 3, ys[3])
+
         for s in range(GROUP):
             for rl in range(4):
                 weigh(last, rl, s, ys[rl])
         turn_h(last - 1, 0)
         turn_h(last - 1, 1)
-        quantize_h(last - 1, 0, GROUP)
-        pair_out = last - OUT_LAG
-        for half in range(2):
-            for s in range(2):
-                second_matmul(2 * (pair_out + half) + s, False)
-            turn_h(last, half)
-            quantize_h(last, 2 * half, 2)
-        for b in range(2 * (pair_out + 2), B):
-            second_matmul(b, b >= B - GROUP)
+        late = last - OUT_LAG + 1
+        second_stage(late)
+        turn_h(last, 0)
+        quantize(last + 1, 0, 512)
+        quantize(last + 2, 0, 256)
+        tags = ["z0", "z1"] + y_tags
+        for k, b in enumerate(range(2 * late + 2, B)):
+            second_matmul(b, tags[k])
+            if k == 1:
+                turn_h(last, 1)
+            add_direct(b)
+            if k == 1:
+                quantize(last + 2, 256, 256)
+                sum_over(late, last + 2)
+                for s in range(2):
+                    add_copied(late, s * N, N)
+            store(b, 1)
+            if k in (3, 5):
+                store(2 * late + k // 4, 1)

@@ -22,7 +22,7 @@ PAIRS = B // 2
 STEPS = 2 * B // GROUP
 X_AHEAD = 3
 XOFF = 1
-OUT_LAG = 4
+OUT_LAG = 3
 ORDER = "aA0bB12QgpDqrHX3s"
 EORDER = "01QpqH23rsX"
 G_COLS = 1024
@@ -34,7 +34,15 @@ EARLY = 4
 WARM = 3
 TAIL = "Ww0HgQw1aAbBKq"
 GB = 8
-XDONE = 10
+WARM2 = 0
+G_TAIL = 1
+T_LAST = 0
+T_EARLY = 1
+T_MID = 1
+T_LATE = 2
+T_FIRST = 0
+TPOS = 0
+XDONE = 11
 
 
 def tile_gated_tensor_train_linear_f1_kernel(
@@ -136,69 +144,68 @@ def tile_gated_tensor_train_linear_f1_kernel(
 
         def quantize(batch, first, count):
             if batch not in codes:
-                codes[batch] = work.tile([P, 1024], U32, name="codes", bufs=7, align_bytes=64)
-                planes[batch] = work.tile([P, 1024], U8, name="plane", bufs=7, align_bytes=64)
+                codes[batch] = work.tile([P, 1024], U32, name="codes", bufs=4, align_bytes=64)
+                planes[batch] = work.tile([P, 1024], U8, name="plane", bufs=4, align_bytes=64)
             nc.vector.quantize_mx(
                 out=codes[batch][:, first : first + count].bitcast(FP8X4),
                 scales=planes[batch][:, first : first + count],
                 in_=grouped[batch][:, 4 * first : 4 * (first + count)],
             )
 
-        def first_matmul(step, rl, tag):
-            group, g = divmod(step, 2)
-            r = 4 * g + rl
-            batch, first = x_place(group)
+        def first_matmul(step, k, tag):
+            batch, first = x_place(step // 2)
+            first = first + 256 * (step % 2)
             y = bank(tag)
-            nc.tensor.matmul_mx(
-                out=y[:],
-                lhsT=a_codes[:, 2 * J * r : 2 * J * (r + 1)].bitcast(FP4X4),
-                lhsT_scale=a_plane[:, J * r : J * (r + 1)],
-                rhs=codes[batch][:, first : first + 512].bitcast(FP8X4),
-                rhs_scale=planes[batch][:, first : first + 512],
-                start=True,
-                stop=True,
-            )
+            for half in range(2):
+                r = 2 * k + half
+                nc.tensor.matmul_mx(
+                    out=y[:, 256 * half : 256 * (half + 1)],
+                    lhsT=a_codes[:, 2 * J * r : 2 * J * (r + 1)].bitcast(FP4X4),
+                    lhsT_scale=a_plane[:, J * r : J * (r + 1)],
+                    rhs=codes[batch][:, first : first + 256].bitcast(FP8X4),
+                    rhs_scale=planes[batch][:, first : first + 256],
+                    start=True,
+                    stop=True,
+                )
             return y
 
-        def weigh(step, rl, s, y):
-            group, g = divmod(step, 2)
-            r = 4 * g + rl
-            col = (GROUP * group + s) * R + r
+        def weigh(step, r, s, y):
+            g, rl = divmod(r, 4)
+            col = (2 * step + s) * R + r
+            first = 256 * (r % 2) + I1 * s
             nc.vector.scalar_tensor_tensor(
-                out=h_rows[step, s // 2][:, s % 2, :, 64 * rl : 64 * (rl + 1)],
-                in0=y[:, s * I1 : (s + 1) * I1].rearrange("p (u m) -> p u m", u=2),
+                out=h_rows[step, s][:, g, :, 64 * rl : 64 * (rl + 1)],
+                in0=y[:, first : first + I1].rearrange("p (u m) -> p u m", u=2),
                 scalar=sig[:, col : col + 1],
                 in1=gain_sb[:, r, :].rearrange("p (u m) -> p u m", u=2),
                 op0=MULT,
                 op1=MULT,
             )
 
-        def turn_h(step, half):
-            ht = bank("ht%d" % half)
-            for s in range(2):
+        def turn_h(step, s):
+            ht = bank("ht%d" % s)
+            for g in range(2):
                 for u in range(2):
-                    col = (2 * s + u) * P
-                    nc.tensor.transpose(
-                        ht[:, col : col + P], h_rows[step, half][:, s, u, :].bitcast(F32), ident[:]
-                    )
+                    col = (2 * g + u) * P
+                    nc.tensor.transpose(ht[:, col : col + P], h_rows[step, s][:, g, u, :].bitcast(F32), ident[:])
             nc.scalar.copy(
-                out=staged(step + 2)[:, half * 1024 : (half + 1) * 1024]
+                out=staged(step + 2)[:, s * 1024 : (s + 1) * 1024]
                 .bitcast(F32)
-                .rearrange("p (s j u) -> p s j u", s=2, u=2),
-                in_=ht[:].rearrange("p (s u j) -> p s j u", s=2, u=2),
+                .rearrange("p (g j u) -> p g j u", g=2, u=2),
+                in_=ht[:].rearrange("p (g u j) -> p g j u", g=2, u=2),
             )
 
         results, summed, zs = {}, {}, {}
 
         def second_matmul(b, tag):
-            group, s = divmod(b, GROUP)
+            batch = b // 2 + 2
             z = bank(tag)
             for g in range(2):
-                batch = 2 * group + g + 2
+                first = (2 * (b % 2) + g) * J
                 nc.tensor.matmul_mx(
                     out=z[:],
-                    lhsT=codes[batch][:, s * J : (s + 1) * J].bitcast(FP8X4),
-                    lhsT_scale=planes[batch][:, s * J : (s + 1) * J],
+                    lhsT=codes[batch][:, first : first + J].bitcast(FP8X4),
+                    lhsT_scale=planes[batch][:, first : first + J],
                     rhs=c_codes[:, g, :].bitcast(FP4X4),
                     rhs_scale=c_plane[:, g, :],
                     start=(g == 0),
@@ -275,20 +282,64 @@ def tile_gated_tensor_train_linear_f1_kernel(
                 second_matmul(b, "z%d" % (b % 2))
                 copy_out(b)
 
-        def weigh_rank(step, rl, y):
-            for s in range(GROUP):
-                weigh(step, rl, s, y)
+        tables, h_whole = {}, {}
 
+        def table_count(step):
+            if step == 0:
+                return T_FIRST
+            if step == STEPS - 1:
+                return T_LAST
+            return T_EARLY if step < OUT_LAG else (T_MID if step < XDONE else T_LATE)
+
+        def make_tables(step):
+            for k in range(4 - table_count(step), 4):
+                table = work.tile([P, 2, 2, 2, 64], F32, name="table", bufs=5)
+                for s in range(2):
+                    for half in range(2):
+                        r = 2 * k + half
+                        col = (2 * step + s) * R + r
+                        nc.scalar.activation(
+                            out=table[:, s, :, half, :],
+                            in_=gain_sb[:, r, :].rearrange("p (u m) -> p u m", u=2),
+                            func=mybir.ActivationFunctionType.Copy,
+                            scale=sig[:, col : col + 1],
+                        )
+                tables[step, k] = table
+
+        def weigh_rank(step, k, y):
+            if (step, k) in tables:
+                g, first = k // 2, 128 * (k % 2)
+                nc.vector.tensor_tensor(
+                    out=h_whole[step][:, :, g, :, first : first + 128].rearrange("p s u (h m) -> p s u h m", h=2),
+                    in0=y[:].rearrange("p (h s u m) -> p s u h m", h=2, s=2, u=2),
+                    in1=tables[step, k][:],
+                    op=MULT,
+                )
+            else:
+                for s in range(2):
+                    for half in range(2):
+                        weigh(step, 2 * k + half, s, y)
+
+        warm = bank("y0")
+        for k in range(WARM2):
+            nc.tensor.matmul(warm[:], lhsT=zeros[:, 0:P], rhs=zeros[:], start=True, stop=True)
         next_x = 2
         y_turn = 0
         last = STEPS - 1
         for step in range(STEPS):
-            for half in range(2):
-                h_rows[step, half] = work.tile([P, 2, 2, 256], BF16, name="h_rows", bufs=6)
+            if step == last:
+                for half in range(2):
+                    h_rows[step, half] = work.tile([P, 2, 2, 256], BF16, name="h_last", bufs=2)
+            else:
+                whole = work.tile([P, 2, 2, 2, 256], BF16, name="h_rows")
+                h_whole[step] = whole
+                for half in range(2):
+                    h_rows[step, half] = whole[:, half, :, :, :]
             pair_out = step - OUT_LAG
             if pair_out < 0:
                 y_tags = ["z0", "y0", "y1", "y2"]
-                ys = [first_matmul(step, rl, y_tags[rl]) for rl in range(2)]
+                ys = [first_matmul(step, rl, y_tags[rl]) for rl in range(2 if step else 4)]
+                make_tables(step)
                 if step > 0:
                     quantize(step, 0, batch_width(step) // 4)
                     turn_h(step - 1, 0)
@@ -297,7 +348,7 @@ def tile_gated_tensor_train_linear_f1_kernel(
                     turn_x(next_x, "ht0")
                     turn_x(next_x + 1, "ht1")
                     next_x = next_x + 2
-                ys.extend([first_matmul(step, rl, y_tags[rl]) for rl in range(2, 4)])
+                ys.extend([first_matmul(step, rl, y_tags[rl]) for rl in range(len(ys), 4)])
                 for rl in range(4):
                     weigh_rank(step, rl, ys[rl])
                 if step > 0:
@@ -306,6 +357,7 @@ def tile_gated_tensor_train_linear_f1_kernel(
                     next_x = next_x + 2
                 continue
             second_stage(pair_out)
+            make_tables(step)
             x_left = next_x < PAIRS
             if x_left or step == XDONE:
                 y_tags = ["y%d" % ((y_turn + rl) % 3) for rl in range(4)]
@@ -329,27 +381,36 @@ def tile_gated_tensor_train_linear_f1_kernel(
                 ys.append(first_matmul(step, 3, y_tags[3]))
             weigh_rank(step, 3, ys[3])
 
-        for s in range(GROUP):
-            for rl in range(4):
-                weigh(last, rl, s, ys[rl])
+        for s in range(2):
+            for r in range(R):
+                weigh(last, r, s, ys[r // 2])
         turn_h(last - 1, 0)
         turn_h(last - 1, 1)
         late = last - OUT_LAG + 1
-        second_stage(late)
+        second_matmul(2 * late, "z0")
         turn_h(last, 0)
+        second_matmul(2 * late + 1, "z1")
+        turn_h(last, 1)
+        for s in range(2 - G_TAIL, 2):
+            copy_out(2 * late + s)
         quantize(last + 1, 0, 512)
         quantize(last + 2, 0, 256)
-        tags = ["z0", "z1"] + y_tags
-        for k, b in enumerate(range(2 * late + 2, B)):
-            second_matmul(b, tags[k])
-            if k == 1:
-                turn_h(last, 1)
+        for s in range(2 - G_TAIL):
+            add_direct(2 * late + s)
+            store(2 * late + s, 1)
+        for b in range(B - 4, B - 2):
+            second_matmul(b, y_tags[b % 4])
+        quantize(last + 2, 256, 256)
+        add_direct(B - 4)
+        store(B - 4, 1)
+        for b in range(B - 2, B):
+            second_matmul(b, y_tags[b % 4])
+        if G_TAIL:
+            sum_over(late, last + 2)
+        for s in range(2 - G_TAIL, 2):
+            add_copied(late, s * N, N)
+        for b in range(B - 3, B):
             add_direct(b)
-            if k == 1:
-                quantize(last + 2, 256, 256)
-                sum_over(late, last + 2)
-                for s in range(2):
-                    add_copied(late, s * N, N)
             store(b, 1)
-            if k in (3, 5):
-                store(2 * late + k // 4, 1)
+            if b - (B - 2) + G_TAIL >= 1 and b < B - 1:
+                store(2 * late + 2 - G_TAIL + (b - (B - 2) + G_TAIL - 1), 1)

@@ -17,32 +17,18 @@ MULT = mybir.AluOpType.mult
 ADD = mybir.AluOpType.add
 
 P = 128
-GROUP = 4
+BANK = 512
 PAIRS = B // 2
-STEPS = 2 * B // GROUP
-X_AHEAD = 3
-XOFF = 1
+Y_BANKS = R // 2
+X_WORDS = 2 * I1
+H_WORDS = 2 * 2 * J
+H_LAG = 2
 OUT_LAG = 3
-ORDER = "aA0bB12QgpDqrHX3s"
-EORDER = "01QpqH23rsX"
-G_COLS = 1024
-Y_BANKS = 3
-Z_BANKS = 2
-TAIL_DIRECT = 4
-SORT = 0
-EARLY = 4
-WARM = 3
-TAIL = "Ww0HgQw1aAbBKq"
-GB = 8
-WARM2 = 0
-G_TAIL = 1
-T_LAST = 0
-T_EARLY = 1
-T_MID = 1
-T_LATE = 2
-T_FIRST = 0
-TPOS = 0
-XDONE = 11
+STAGES = 8
+GPSIMD_COLS = 832
+TABLES_BESIDE_X = 1
+TABLES_AFTER_X = 2
+WARM_UPS = 3
 
 
 def tile_gated_tensor_train_linear_f1_kernel(
@@ -56,125 +42,124 @@ def tile_gated_tensor_train_linear_f1_kernel(
         ctx.enter_context(tc.manual_schedule())
 
         def bank(tag):
-            return psum.tile([P, 512], F32, name=tag, tag=tag)
+            return psum.tile([P, BANK], F32, name=tag, tag=tag)
 
-        a_plane = keep.tile([P, R * J], U8, align_bytes=64)
-        c_plane = keep.tile([P, 2, N], U8, align_bytes=64)
-        rows = keep.tile([P, 256], BF16)
-        zeros = keep.tile([P, 512], BF16)
+        zeros = keep.tile([P, BANK], BF16)
+        rows = keep.tile([P, B * R], BF16)
+        a_scale_tile = keep.tile([P, R * J], U8, align_bytes=64)
+        c_scale_tile = keep.tile([P, 2, N], U8, align_bytes=64)
         nc.vector.memset(zeros[:].bitcast(I32), 0)
         nc.vector.memset(rows[:].bitcast(I32), 0)
-        nc.vector.memset(a_plane[:].bitcast(I32), 0)
-        nc.vector.memset(c_plane[:].rearrange("p g n -> p (g n)").bitcast(I32), 0)
+        nc.vector.memset(a_scale_tile[:].bitcast(I32), 0)
+        nc.vector.memset(c_scale_tile[:].rearrange("p g n -> p (g n)").bitcast(I32), 0)
         ident = keep.tile([P, P], F32)
         make_identity(nc, ident[:])
 
+        a_codes = keep.tile([P, 2 * R * J], U8, align_bytes=64)
+        c_codes = keep.tile([P, 2, 2 * N], U8, align_bytes=64)
+        bias_raw = keep.tile([P, N], BF16)
         x_sb = []
 
         def load_x(pair):
-            t = keep.tile([P, 2, I2], BF16, name="x%d" % pair)
-            nc.sync.dma_start(out=t[:], in_=x[2 * pair : 2 * pair + 2].rearrange("b i c -> i b c"))
-            x_sb.append(t)
-
-        a_codes = keep.tile([P, 2 * R * J], U8, align_bytes=64)
-        c_codes = keep.tile([P, 2, 2 * N], U8, align_bytes=64)
-        bias_sb = keep.tile([P, 2, N], BF16)
+            x_pair = keep.tile([P, 2, I2], BF16, name="x%d" % pair)
+            nc.sync.dma_start(out=x_pair[:], in_=x[2 * pair : 2 * pair + 2].rearrange("b i c -> i b c"))
+            x_sb.append(x_pair)
 
         load_x(0)
         nc.sync.dma_start(out=rows[0:R, 0:I1], in_=gain)
         nc.sync.dma_start(out=rows[R : R + 1, :], in_=gate.rearrange("(o b) r -> o (b r)", o=1))
         load_x(1)
         nc.sync.dma_start(out=a_codes[:].bitcast(I32), in_=a_words[0].bitcast(I32))
-        for q in range(4):
+        for quadrant in range(4):
             nc.sync.dma_start(
-                out=a_plane[32 * q : 32 * q + 4, :].bitcast(I32),
-                in_=a_scales[0, 4 * q : 4 * q + 4, :].bitcast(I32),
+                out=a_scale_tile[32 * quadrant : 32 * quadrant + 4, :].bitcast(I32),
+                in_=a_scales[0, 4 * quadrant : 4 * quadrant + 4, :].bitcast(I32),
             )
-        load_x(2)
-        load_x(3)
-        load_x(4)
+        x_before_c = 5
+        for pair in range(2, x_before_c):
+            load_x(pair)
         nc.sync.dma_start(out=c_codes[:].bitcast(I32), in_=c_words.rearrange("g p n -> p g n").bitcast(I32))
-        for q in range(4):
+        for quadrant in range(4):
             nc.sync.dma_start(
-                out=c_plane[32 * q : 32 * q + 4, :, :].bitcast(I32),
-                in_=c_scales[:, 4 * q : 4 * q + 4, :].rearrange("g s n -> s g n").bitcast(I32),
+                out=c_scale_tile[32 * quadrant : 32 * quadrant + 4, :, :].bitcast(I32),
+                in_=c_scales[:, 4 * quadrant : 4 * quadrant + 4, :].rearrange("g s n -> s g n").bitcast(I32),
             )
-        for s in range(2):
-            nc.sync.dma_start(out=bias_sb[:, s, :], in_=bias)
-        for pair in range(5, PAIRS):
+        nc.sync.dma_start(out=bias_raw[:], in_=bias)
+        for pair in range(x_before_c, PAIRS):
             load_x(pair)
 
-        grouped, codes, planes, h_rows = {}, {}, {}, {}
+        staging, codes, scales = {}, {}, {}
 
-        def batch_width(batch):
-            group = (batch + XOFF) // 2
-            return (2048 if batch >= 2 else 0) + (2048 if (batch + XOFF) % 2 == 0 and 0 < group < B // GROUP else 0)
+        def stage_tag(step):
+            return "stage%d" % (step % STAGES)
 
-        def staged(batch):
-            if batch not in grouped:
-                grouped[batch] = work.tile([P, 4096], BF16, name="grouped", tag="stage%d" % (batch % GB), bufs=1, align_bytes=64)
-            return grouped[batch]
+        def staged(step):
+            if step not in staging:
+                staging[step] = work.tile(
+                    [P, 4 * (H_WORDS + 2 * X_WORDS)], BF16, name="staging", tag=stage_tag(step), bufs=1, align_bytes=64
+                )
+            return staging[step]
 
-        def x_place(group):
-            batch = 2 * group - XOFF
-            return batch, (512 if batch >= 2 else 0)
+        def x_place(pair):
+            step = pair - pair % 2 - 1
+            return step, (H_WORDS if step >= H_LAG else 0) + X_WORDS * (pair % 2)
+
+        def step_words(step):
+            has_x = step % 2 == 1 and step + 1 < PAIRS
+            return (H_WORDS if step >= H_LAG else 0) + (2 * X_WORDS if has_x else 0)
+
+        def quantize(step, first, count):
+            if step not in codes:
+                codes[step] = work.tile([P, H_WORDS + 2 * X_WORDS], U32, name="codes", bufs=4, align_bytes=64)
+                scales[step] = work.tile([P, H_WORDS + 2 * X_WORDS], U8, name="scales", bufs=4, align_bytes=64)
+            nc.vector.quantize_mx(
+                out=codes[step][:, first : first + count].bitcast(FP8X4),
+                scales=scales[step][:, first : first + count],
+                in_=staging[step][:, 4 * first : 4 * (first + count)],
+            )
 
         def turn_x(pair, tag):
             xt = bank(tag)
-            if SORT:
-                srt = work.tile([P, 2, 2, P], U32, name="x_sorted")
-                nc.scalar.copy(out=srt[:], in_=x_sb[pair][:].bitcast(U32).rearrange("p s (m w) -> p s w m", w=2))
             for s in range(2):
-                words = x_sb[pair][:, s, :].bitcast(F32)
+                duos = x_sb[pair][:, s, :].bitcast(F32)
                 for w in range(2):
                     col = (2 * s + w) * P
-                    if SORT:
-                        nc.tensor.transpose(xt[:, col : col + P], srt[:, s, w, :].bitcast(F32), ident[:])
-                    else:
-                        nc.tensor.transpose(xt[:, col : col + P], words[:, w : 2 * P : 2], ident[:])
-            batch, first = x_place(pair // 2)
+                    nc.tensor.transpose(xt[:, col : col + P], duos[:, w : 2 * P : 2], ident[:])
+            step, first = x_place(pair)
             for s in range(2):
-                col = 4 * (first + (2 * (pair % 2) + s) * I1)
+                col = 4 * (first + s * I1)
                 nc.scalar.copy(
-                    out=staged(batch)[:, col : col + 512]
+                    out=staged(step)[:, col : col + 4 * I1]
                     .bitcast(F32)
                     .rearrange("p (u q e w) -> p u q e w", u=2, e=2, w=2),
-                    in_=xt[:, s * 256 : (s + 1) * 256].rearrange("p (w q u e) -> p u q e w", w=2, u=2, e=2),
+                    in_=xt[:, s * 2 * P : (s + 1) * 2 * P].rearrange("p (w q u e) -> p u q e w", w=2, u=2, e=2),
                 )
 
-        def quantize(batch, first, count):
-            if batch not in codes:
-                codes[batch] = work.tile([P, 1024], U32, name="codes", bufs=4, align_bytes=64)
-                planes[batch] = work.tile([P, 1024], U8, name="plane", bufs=4, align_bytes=64)
-            nc.vector.quantize_mx(
-                out=codes[batch][:, first : first + count].bitcast(FP8X4),
-                scales=planes[batch][:, first : first + count],
-                in_=grouped[batch][:, 4 * first : 4 * (first + count)],
-            )
+        sig = keep.tile([P, B * R], F32)
+        gain_sb = keep.tile([P, R, I1], BF16)
+        h_pair, h_rows, tables = {}, {}, {}
 
-        def first_matmul(step, k, tag):
-            batch, first = x_place(step // 2)
-            first = first + 256 * (step % 2)
+        def first_matmul(pair, k, tag):
+            step, first = x_place(pair)
             y = bank(tag)
             for half in range(2):
                 r = 2 * k + half
                 nc.tensor.matmul_mx(
-                    out=y[:, 256 * half : 256 * (half + 1)],
+                    out=y[:, X_WORDS * half : X_WORDS * (half + 1)],
                     lhsT=a_codes[:, 2 * J * r : 2 * J * (r + 1)].bitcast(FP4X4),
-                    lhsT_scale=a_plane[:, J * r : J * (r + 1)],
-                    rhs=codes[batch][:, first : first + 256].bitcast(FP8X4),
-                    rhs_scale=planes[batch][:, first : first + 256],
+                    lhsT_scale=a_scale_tile[:, J * r : J * (r + 1)],
+                    rhs=codes[step][:, first : first + X_WORDS].bitcast(FP8X4),
+                    rhs_scale=scales[step][:, first : first + X_WORDS],
                     start=True,
                     stop=True,
                 )
             return y
 
-        def weigh(step, r, s, y):
-            g, rl = divmod(r, 4)
-            col = (2 * step + s) * R + r
-            first = 256 * (r % 2) + I1 * s
+        def weigh_one(pair, r, s, y):
+            col = (2 * pair + s) * R + r
+            first = X_WORDS * (r % 2) + I1 * s
             nc.vector.scalar_tensor_tensor(
-                out=h_rows[step, s][:, g, :, 64 * rl : 64 * (rl + 1)],
+                out=h_rows[pair, s][:, r // 4, :, 64 * (r % 4) : 64 * (r % 4 + 1)],
                 in0=y[:, first : first + I1].rearrange("p (u m) -> p u m", u=2),
                 scalar=sig[:, col : col + 1],
                 in1=gain_sb[:, r, :].rearrange("p (u m) -> p u m", u=2),
@@ -182,235 +167,209 @@ def tile_gated_tensor_train_linear_f1_kernel(
                 op1=MULT,
             )
 
-        def turn_h(step, s):
-            ht = bank("ht%d" % s)
-            for g in range(2):
-                for u in range(2):
-                    col = (2 * g + u) * P
-                    nc.tensor.transpose(ht[:, col : col + P], h_rows[step, s][:, g, u, :].bitcast(F32), ident[:])
-            nc.scalar.copy(
-                out=staged(step + 2)[:, s * 1024 : (s + 1) * 1024]
-                .bitcast(F32)
-                .rearrange("p (g j u) -> p g j u", g=2, u=2),
-                in_=ht[:].rearrange("p (g u j) -> p g j u", g=2, u=2),
-            )
-
-        results, summed, zs = {}, {}, {}
-
-        def second_matmul(b, tag):
-            batch = b // 2 + 2
-            z = bank(tag)
-            for g in range(2):
-                first = (2 * (b % 2) + g) * J
-                nc.tensor.matmul_mx(
-                    out=z[:],
-                    lhsT=codes[batch][:, first : first + J].bitcast(FP8X4),
-                    lhsT_scale=planes[batch][:, first : first + J],
-                    rhs=c_codes[:, g, :].bitcast(FP4X4),
-                    rhs_scale=c_plane[:, g, :],
-                    start=(g == 0),
-                    stop=(g == 1),
-                )
-            zs[b] = z
-            if b % 2 == 0:
-                results[b // 2] = work.tile([P, 2 * N], F32, name="result", bufs=4)
-
-        def copy_out(b):
-            base = (b % 2) * N
-            nc.scalar.copy(out=results[b // 2][:, base : base + N], in_=zs[b][:])
-
-        def add_direct(b):
-            base = (b % 2) * N
-            summed[b // 2] = results[b // 2]
-            nc.vector.tensor_tensor(out=results[b // 2][:, base : base + N], in0=zs[b][:], in1=bias_sb[:, 0, :], op=ADD)
-
-        def add_copied(pair, first, count):
-            nc.gpsimd.tensor_tensor(
-                out=summed[pair][:, first : first + count],
-                in0=results[pair][:, first : first + count],
-                in1=bias_sb[:].rearrange("p s n -> p (s n)")[:, first : first + count],
-                op=ADD,
-            )
-
-        def store(first, count):
-            base = (first % 2) * N
-            nc.sync.dma_start(
-                out=out[first : first + count].rearrange("b j n -> j b n"),
-                in_=summed[first // 2][:, base : base + count * N].rearrange("p (s n) -> p s n", s=count),
-            )
-
-        warm = bank("y0")
-        for k in range(WARM):
-            nc.tensor.matmul(warm[:], lhsT=zeros[:, 0:P], rhs=zeros[:], start=True, stop=True)
-        turn_x(0, "ht0")
-        turn_x(1, "ht1")
-        pick = keep.tile([P, 16], BF16)
-        nc.vector.tensor_copy(out=pick[:], in_=ident[:, 0:16])
-        quantize(-XOFF, 0, 256)
-        quantize(-XOFF, 256, 256)
-        sig = keep.tile([P, B * R], F32)
-        gain_sb = keep.tile([P, R, I1], BF16)
-        spread = bank("xt")
-        nc.tensor.matmul(
-            spread[:, 0 : B * R], lhsT=pick[:, R : R + 1].to_broadcast([P, P]), rhs=rows[:], start=True, stop=True
-        )
-        nc.scalar.activation(out=sig[:], in_=spread[:, 0 : B * R], func=mybir.ActivationFunctionType.Sigmoid)
-        for half in range(2):
-            spread = bank(["y2", "z1"][half])
-            for rl in range(4):
-                r = 4 * half + rl
-                nc.tensor.matmul(
-                    spread[:, rl * I1 : (rl + 1) * I1],
-                    lhsT=pick[:, r : r + 1].to_broadcast([P, P]),
-                    rhs=rows[:, 0:I1],
-                    start=True,
-                    stop=True,
-                )
-            copy = nc.scalar.copy if half else nc.vector.tensor_copy
-            copy(
-                out=gain_sb[:, 4 * half : 4 * half + 4, :].rearrange("p r (u q e) -> p r u q e", u=2, e=2),
-                in_=spread[:].rearrange("p (r q u e) -> p r u q e", r=4, u=2, e=2),
-            )
-
-        def sum_over(pair, batch):
-            summed[pair] = work.tile(
-                [P, 2 * N], F32, name="summed", tag="stage%d" % (batch % GB), bufs=1, align_bytes=64
-            )
-
-        def second_stage(pair):
-            for b in (2 * pair, 2 * pair + 1):
-                second_matmul(b, "z%d" % (b % 2))
-                copy_out(b)
-
-        tables, h_whole = {}, {}
-
-        def table_count(step):
-            if step == 0:
-                return T_FIRST
-            if step == STEPS - 1:
-                return T_LAST
-            return T_EARLY if step < OUT_LAG else (T_MID if step < XDONE else T_LATE)
-
-        def make_tables(step):
-            for k in range(4 - table_count(step), 4):
+        def make_tables(pair, count):
+            for k in range(Y_BANKS - count, Y_BANKS):
                 table = work.tile([P, 2, 2, 2, 64], F32, name="table", bufs=5)
                 for s in range(2):
                     for half in range(2):
                         r = 2 * k + half
-                        col = (2 * step + s) * R + r
+                        col = (2 * pair + s) * R + r
                         nc.scalar.activation(
                             out=table[:, s, :, half, :],
                             in_=gain_sb[:, r, :].rearrange("p (u m) -> p u m", u=2),
                             func=mybir.ActivationFunctionType.Copy,
                             scale=sig[:, col : col + 1],
                         )
-                tables[step, k] = table
+                tables[pair, k] = table
 
-        def weigh_rank(step, k, y):
-            if (step, k) in tables:
-                g, first = k // 2, 128 * (k % 2)
+        def weigh_bank(pair, k, y):
+            if (pair, k) in tables:
+                first = 128 * (k % 2)
                 nc.vector.tensor_tensor(
-                    out=h_whole[step][:, :, g, :, first : first + 128].rearrange("p s u (h m) -> p s u h m", h=2),
+                    out=h_pair[pair][:, :, k // 2, :, first : first + 128].rearrange("p s u (h m) -> p s u h m", h=2),
                     in0=y[:].rearrange("p (h s u m) -> p s u h m", h=2, s=2, u=2),
-                    in1=tables[step, k][:],
+                    in1=tables[pair, k][:],
                     op=MULT,
                 )
             else:
                 for s in range(2):
                     for half in range(2):
-                        weigh(step, 2 * k + half, s, y)
+                        weigh_one(pair, 2 * k + half, s, y)
+
+        def turn_h(pair, s):
+            ht = bank("ht%d" % s)
+            for g in range(2):
+                for u in range(2):
+                    col = (2 * g + u) * P
+                    nc.tensor.transpose(ht[:, col : col + P], h_rows[pair, s][:, g, u, :].bitcast(F32), ident[:])
+            nc.scalar.copy(
+                out=staged(pair + H_LAG)[:, s * 8 * J : (s + 1) * 8 * J]
+                .bitcast(F32)
+                .rearrange("p (g j u) -> p g j u", g=2, u=2),
+                in_=ht[:].rearrange("p (g u j) -> p g j u", g=2, u=2),
+            )
+
+        bias_sb = keep.tile([P, 2 * N], F32)
+        z_banks = {}
+
+        def second_matmul(b, tag):
+            step = b // 2 + H_LAG
+            z = bank(tag)
+            for g in range(2):
+                first = (2 * (b % 2) + g) * J
+                nc.tensor.matmul_mx(
+                    out=z[:],
+                    lhsT=codes[step][:, first : first + J].bitcast(FP8X4),
+                    lhsT_scale=scales[step][:, first : first + J],
+                    rhs=c_codes[:, g, :].bitcast(FP4X4),
+                    rhs_scale=c_scale_tile[:, g, :],
+                    start=(g == 0),
+                    stop=(g == 1),
+                )
+            z_banks[b] = z
+
+        def pair_tile():
+            return work.tile([P, 2 * N], F32, name="pair_tile", bufs=4)
+
+        def over_staging(step):
+            return work.tile([P, 2 * N], F32, name="summed", tag=stage_tag(step), bufs=1, align_bytes=64)
+
+        def add_on_gpsimd(summed, copied, first, count):
+            cols = slice(first, first + count)
+            nc.gpsimd.tensor_tensor(out=summed[:, cols], in0=copied[:, cols], in1=bias_sb[:, cols], op=ADD)
+
+        def add_on_vector(summed, b, first):
+            base = (b % 2) * N
+            nc.vector.tensor_tensor(
+                out=summed[:, base + first : base + N], in0=z_banks[b][:, first:N], in1=bias_sb[:, first:N], op=ADD
+            )
+
+        def store(summed, b, count):
+            base = (b % 2) * N
+            nc.sync.dma_start(
+                out=out[b : b + count].rearrange("b j n -> j b n"),
+                in_=summed[:, base : base + count * N].rearrange("p (s n) -> p s n", s=count),
+            )
 
         warm = bank("y0")
-        for k in range(WARM2):
+        for k in range(WARM_UPS):
             nc.tensor.matmul(warm[:], lhsT=zeros[:, 0:P], rhs=zeros[:], start=True, stop=True)
-        next_x = 2
-        y_turn = 0
-        last = STEPS - 1
-        for step in range(STEPS):
-            if step == last:
-                for half in range(2):
-                    h_rows[step, half] = work.tile([P, 2, 2, 256], BF16, name="h_last", bufs=2)
-            else:
-                whole = work.tile([P, 2, 2, 2, 256], BF16, name="h_rows")
-                h_whole[step] = whole
-                for half in range(2):
-                    h_rows[step, half] = whole[:, half, :, :, :]
-            pair_out = step - OUT_LAG
-            if pair_out < 0:
-                y_tags = ["z0", "y0", "y1", "y2"]
-                ys = [first_matmul(step, rl, y_tags[rl]) for rl in range(2 if step else 4)]
-                make_tables(step)
-                if step > 0:
-                    quantize(step, 0, batch_width(step) // 4)
-                    turn_h(step - 1, 0)
-                    turn_h(step - 1, 1)
-                else:
-                    turn_x(next_x, "ht0")
-                    turn_x(next_x + 1, "ht1")
-                    next_x = next_x + 2
-                ys.extend([first_matmul(step, rl, y_tags[rl]) for rl in range(len(ys), 4)])
-                for rl in range(4):
-                    weigh_rank(step, rl, ys[rl])
-                if step > 0:
-                    turn_x(next_x, "xt")
-                    turn_x(next_x + 1, "z1")
-                    next_x = next_x + 2
-                continue
-            second_stage(pair_out)
-            make_tables(step)
-            x_left = next_x < PAIRS
-            if x_left or step == XDONE:
-                y_tags = ["y%d" % ((y_turn + rl) % 3) for rl in range(4)]
-                y_turn = y_turn + 4
-                if not x_left:
-                    y_tags[3] = "xt"
-            ys = [first_matmul(step, rl, y_tags[rl]) for rl in range(3 if x_left else 4)]
-            quantize(step, 0, batch_width(step) // 4)
-            sum_over(pair_out, step)
-            add_copied(pair_out, 0, 2 * N)
-            store(2 * pair_out, 2)
-            if step == last:
-                break
-            for rl in range(3):
-                weigh_rank(step, rl, ys[rl])
+        turn_x(0, "ht0")
+        pick = keep.tile([P, 2 * R], BF16)
+        nc.vector.tensor_copy(out=pick[:], in_=ident[:, 0 : 2 * R])
+        quantize(-1, 0, X_WORDS)
+        spread = bank("xt")
+        nc.tensor.matmul(
+            spread[:, 0 : B * R], lhsT=pick[:, R : R + 1].to_broadcast([P, P]), rhs=rows[:], start=True, stop=True
+        )
+        nc.scalar.activation(out=sig[:], in_=spread[:, 0 : B * R], func=mybir.ActivationFunctionType.Sigmoid)
+        for g, (tag, copy) in enumerate((("y2", nc.vector.tensor_copy), ("z1", nc.scalar.copy))):
+            spread = bank(tag)
+            for rl in range(4):
+                nc.tensor.matmul(
+                    spread[:, rl * I1 : (rl + 1) * I1],
+                    lhsT=pick[:, 4 * g + rl : 4 * g + rl + 1].to_broadcast([P, P]),
+                    rhs=rows[:, 0:I1],
+                    start=True,
+                    stop=True,
+                )
+            copy(
+                out=gain_sb[:, 4 * g : 4 * g + 4, :].rearrange("p r (u q e) -> p r u q e", u=2, e=2),
+                in_=spread[:].rearrange("p (r q u e) -> p r u q e", r=4, u=2, e=2),
+            )
+
+        def new_h(pair):
+            h_pair[pair] = work.tile([P, 2, 2, 2, 256], BF16, name="h_pair")
+            for s in range(2):
+                h_rows[pair, s] = h_pair[pair][:, s, :, :, :]
+
+        early_tags = ["z0", "y0", "y1", "y2"]
+        new_h(0)
+        turn_x(1, "ht1")
+        ys = [first_matmul(0, k, early_tags[k]) for k in range(Y_BANKS)]
+        turn_x(2, "ht0")
+        turn_x(3, "ht1")
+        weigh_bank(0, 0, ys[0])
+        quantize(-1, X_WORDS, X_WORDS)
+        for k in range(1, Y_BANKS):
+            weigh_bank(0, k, ys[k])
+        for step in range(1, OUT_LAG):
+            new_h(step)
+            ys = [first_matmul(step, k, early_tags[k]) for k in range(2)]
+            make_tables(step, TABLES_BESIDE_X)
+            quantize(step, 0, step_words(step))
             turn_h(step - 1, 0)
             turn_h(step - 1, 1)
-            if x_left:
-                turn_x(next_x, "xt")
-                next_x = next_x + 1
-                ys.append(first_matmul(step, 3, y_tags[3]))
-            weigh_rank(step, 3, ys[3])
+            ys.extend([first_matmul(step, k, early_tags[k]) for k in range(2, Y_BANKS)])
+            for k in range(Y_BANKS):
+                weigh_bank(step, k, ys[k])
+            if step == OUT_LAG - 2:
+                for s in range(2):
+                    nc.scalar.copy(out=bias_sb[:, s * N : (s + 1) * N], in_=bias_raw[:])
+            turn_x(2 * step + 2, "xt")
+            turn_x(2 * step + 3, "z1")
+
+        x_ahead = OUT_LAG + 2
+        last = PAIRS - 1
+        for step in range(OUT_LAG, PAIRS):
+            x_left = step + x_ahead < PAIRS
+            done = step - OUT_LAG
+            copied = pair_tile()
+            for s, count in enumerate((N, GPSIMD_COLS - N)):
+                second_matmul(2 * done + s, "z%d" % s)
+                nc.scalar.copy(out=copied[:, s * N : s * N + count], in_=z_banks[2 * done + s][:, 0:count])
+            if step < last:
+                new_h(step)
+                make_tables(step, TABLES_BESIDE_X if x_left else TABLES_AFTER_X)
+            if step + x_ahead <= PAIRS:
+                y_tags = ["y%d" % ((step - OUT_LAG + k) % 3) for k in range(3)]
+                y_tags.append(y_tags[0] if x_left else "xt")
+            ys = [first_matmul(step, k, y_tags[k]) for k in range(3 if x_left else Y_BANKS)]
+            quantize(step, 0, step_words(step))
+            summed = over_staging(step)
+            add_on_gpsimd(summed, copied, 0, GPSIMD_COLS)
+            if step < last:
+                weigh_bank(step, 0, ys[0])
+            add_on_vector(summed, 2 * done + 1, GPSIMD_COLS - N)
+            store(summed, 2 * done, 2)
+            if step < last:
+                weigh_bank(step, 1, ys[1])
+                weigh_bank(step, 2, ys[2])
+                turn_h(step - 1, 0)
+                turn_h(step - 1, 1)
+                if x_left:
+                    turn_x(step + x_ahead, "xt")
+                    ys.append(first_matmul(step, 3, y_tags[3]))
+                weigh_bank(step, 3, ys[3])
 
         for s in range(2):
+            h_rows[last, s] = work.tile([P, 2, 2, 256], BF16, name="h_last", bufs=2)
             for r in range(R):
-                weigh(last, r, s, ys[r // 2])
+                weigh_one(last, r, s, ys[r // 2])
         turn_h(last - 1, 0)
         turn_h(last - 1, 1)
-        late = last - OUT_LAG + 1
-        second_matmul(2 * late, "z0")
-        turn_h(last, 0)
-        second_matmul(2 * late + 1, "z1")
-        turn_h(last, 1)
-        for s in range(2 - G_TAIL, 2):
-            copy_out(2 * late + s)
-        quantize(last + 1, 0, 512)
-        quantize(last + 2, 0, 256)
-        for s in range(2 - G_TAIL):
-            add_direct(2 * late + s)
-            store(2 * late + s, 1)
-        for b in range(B - 4, B - 2):
-            second_matmul(b, y_tags[b % 4])
-        quantize(last + 2, 256, 256)
-        add_direct(B - 4)
-        store(B - 4, 1)
-        for b in range(B - 2, B):
-            second_matmul(b, y_tags[b % 4])
-        if G_TAIL:
-            sum_over(late, last + 2)
-        for s in range(2 - G_TAIL, 2):
-            add_copied(late, s * N, N)
-        for b in range(B - 3, B):
-            add_direct(b)
-            store(b, 1)
-            if b - (B - 2) + G_TAIL >= 1 and b < B - 1:
-                store(2 * late + 2 - G_TAIL + (b - (B - 2) + G_TAIL - 1), 1)
+        for s in range(2):
+            second_matmul(B - 6 + s, "z%d" % s)
+            turn_h(last, s)
+        results = [pair_tile() for k in range(3)]
+        nc.scalar.copy(out=results[0][:, N : 2 * N], in_=z_banks[B - 5][:])
+        quantize(last + 1, 0, H_WORDS)
+        quantize(last + 2, 0, H_WORDS // 2)
+        add_on_vector(results[0], B - 6, 0)
+        store(results[0], B - 6, 1)
+        for s in range(2):
+            second_matmul(B - 4 + s, y_tags[s])
+        quantize(last + 2, H_WORDS // 2, H_WORDS // 2)
+        add_on_vector(results[1], B - 4, 0)
+        store(results[1], B - 4, 1)
+        for s in range(2):
+            second_matmul(B - 2 + s, y_tags[2 + s])
+        summed = over_staging(last + 2)
+        add_on_gpsimd(summed, results[0], N, N)
+        add_on_vector(results[1], B - 3, 0)
+        store(results[1], B - 3, 1)
+        add_on_vector(results[2], B - 2, 0)
+        store(results[2], B - 2, 1)
+        store(summed, B - 5, 1)
+        add_on_vector(results[2], B - 1, 0)
+        store(results[2], B - 1, 1)

from contextlib import ExitStack

import concourse.mybir as mybir
from concourse.masks import make_identity

B, I1, I2, R, J, N = 32, 128, 512, 8, 128, 512
FLOPS = 2 * B * I1 * I2 * R * J + 2 * B * J * R * I1 * N

F32 = mybir.dt.float32
BF16 = mybir.dt.bfloat16
I32 = mybir.dt.int32
U32 = mybir.dt.uint32
U8 = mybir.dt.uint8
FP8X4 = mybir.dt.float8_e4m3fn_x4
FP4X4 = mybir.dt.float4_e2m1fn_x4
MULT = mybir.AluOpType.mult
ADD = mybir.AluOpType.add

P = 128
BANK = 512
PAIRS = B // 2
Y_BANKS = R // 2
X_WORDS = 2 * I1
H_WORDS = 2 * 2 * J
H_LAG = 2
OUT_LAG = 3
STAGES = 8
GPSIMD_COLS = 832
TABLES_BESIDE_X = 1
TABLES_AFTER_X = 2
WARM_UPS = 3


def tile_gated_tensor_train_linear_f1_kernel(
    tc, x, a_words, a_scales, gate, gain, c_words, c_scales, bias, out
):
    nc = tc.nc
    with ExitStack() as ctx:
        keep = ctx.enter_context(tc.tile_pool(name="keep", bufs=1))
        work = ctx.enter_context(tc.tile_pool(name="work", bufs=3))
        psum = ctx.enter_context(tc.psum_pool(name="psum", bufs=1))
        ctx.enter_context(tc.manual_schedule())

        def bank(tag):
            return psum.tile([P, BANK], F32, name=tag, tag=tag)

        zeros = keep.tile([P, BANK], BF16)
        rows = keep.tile([P, B * R], BF16)
        a_scale_tile = keep.tile([P, R * J], U8, align_bytes=64)
        c_scale_tile = keep.tile([P, 2, N], U8, align_bytes=64)
        nc.vector.memset(zeros[:].bitcast(I32), 0)
        nc.vector.memset(rows[:].bitcast(I32), 0)
        nc.vector.memset(a_scale_tile[:].bitcast(I32), 0)
        nc.vector.memset(c_scale_tile[:].rearrange("p g n -> p (g n)").bitcast(I32), 0)
        ident = keep.tile([P, P], F32)
        make_identity(nc, ident[:])

        a_codes = keep.tile([P, 2 * R * J], U8, align_bytes=64)
        c_codes = keep.tile([P, 2, 2 * N], U8, align_bytes=64)
        bias_raw = keep.tile([P, N], BF16)
        x_sb = []

        def load_x(pair):
            x_pair = keep.tile([P, 2, I2], BF16, name="x%d" % pair)
            nc.sync.dma_start(out=x_pair[:], in_=x[2 * pair : 2 * pair + 2].rearrange("b i c -> i b c"))
            x_sb.append(x_pair)

        load_x(0)
        nc.sync.dma_start(out=rows[0:R, 0:I1], in_=gain)
        nc.sync.dma_start(out=rows[R : R + 1, :], in_=gate.rearrange("(o b) r -> o (b r)", o=1))
        load_x(1)
        nc.sync.dma_start(out=a_codes[:].bitcast(I32), in_=a_words[0].bitcast(I32))
        for quadrant in range(4):
            nc.sync.dma_start(
                out=a_scale_tile[32 * quadrant : 32 * quadrant + 4, :].bitcast(I32),
                in_=a_scales[0, 4 * quadrant : 4 * quadrant + 4, :].bitcast(I32),
            )
        x_before_c = 5
        for pair in range(2, x_before_c):
            load_x(pair)
        nc.sync.dma_start(out=c_codes[:].bitcast(I32), in_=c_words.rearrange("g p n -> p g n").bitcast(I32))
        for quadrant in range(4):
            nc.sync.dma_start(
                out=c_scale_tile[32 * quadrant : 32 * quadrant + 4, :, :].bitcast(I32),
                in_=c_scales[:, 4 * quadrant : 4 * quadrant + 4, :].rearrange("g s n -> s g n").bitcast(I32),
            )
        nc.sync.dma_start(out=bias_raw[:], in_=bias)
        for pair in range(x_before_c, PAIRS):
            load_x(pair)

        staging, codes, scales = {}, {}, {}

        def stage_tag(step):
            return "stage%d" % (step % STAGES)

        def staged(step):
            if step not in staging:
                staging[step] = work.tile(
                    [P, 4 * (H_WORDS + 2 * X_WORDS)], BF16, name="staging", tag=stage_tag(step), bufs=1, align_bytes=64
                )
            return staging[step]

        def x_place(pair):
            step = pair - pair % 2 - 1
            return step, (H_WORDS if step >= H_LAG else 0) + X_WORDS * (pair % 2)

        def step_words(step):
            has_x = step % 2 == 1 and step + 1 < PAIRS
            return (H_WORDS if step >= H_LAG else 0) + (2 * X_WORDS if has_x else 0)

        def quantize(step, first, count):
            if step not in codes:
                codes[step] = work.tile([P, H_WORDS + 2 * X_WORDS], U32, name="codes", bufs=4, align_bytes=64)
                scales[step] = work.tile([P, H_WORDS + 2 * X_WORDS], U8, name="scales", bufs=4, align_bytes=64)
            nc.vector.quantize_mx(
                out=codes[step][:, first : first + count].bitcast(FP8X4),
                scales=scales[step][:, first : first + count],
                in_=staging[step][:, 4 * first : 4 * (first + count)],
            )

        def turn_x(pair, tag):
            xt = bank(tag)
            for s in range(2):
                duos = x_sb[pair][:, s, :].bitcast(F32)
                for w in range(2):
                    col = (2 * s + w) * P
                    nc.tensor.transpose(xt[:, col : col + P], duos[:, w : 2 * P : 2], ident[:])
            step, first = x_place(pair)
            for s in range(2):
                col = 4 * (first + s * I1)
                nc.scalar.copy(
                    out=staged(step)[:, col : col + 4 * I1]
                    .bitcast(F32)
                    .rearrange("p (u q e w) -> p u q e w", u=2, e=2, w=2),
                    in_=xt[:, s * 2 * P : (s + 1) * 2 * P].rearrange("p (w q u e) -> p u q e w", w=2, u=2, e=2),
                )

        sig = keep.tile([P, B * R], F32)
        gain_sb = keep.tile([P, R, I1], BF16)
        h_pair, h_rows, tables = {}, {}, {}

        def first_matmul(pair, k, tag):
            step, first = x_place(pair)
            y = bank(tag)
            for half in range(2):
                r = 2 * k + half
                nc.tensor.matmul_mx(
                    out=y[:, X_WORDS * half : X_WORDS * (half + 1)],
                    lhsT=a_codes[:, 2 * J * r : 2 * J * (r + 1)].bitcast(FP4X4),
                    lhsT_scale=a_scale_tile[:, J * r : J * (r + 1)],
                    rhs=codes[step][:, first : first + X_WORDS].bitcast(FP8X4),
                    rhs_scale=scales[step][:, first : first + X_WORDS],
                    start=True,
                    stop=True,
                )
            return y

        def weigh_one(pair, r, s, y):
            col = (2 * pair + s) * R + r
            first = X_WORDS * (r % 2) + I1 * s
            nc.vector.scalar_tensor_tensor(
                out=h_rows[pair, s][:, r // 4, :, 64 * (r % 4) : 64 * (r % 4 + 1)],
                in0=y[:, first : first + I1].rearrange("p (u m) -> p u m", u=2),
                scalar=sig[:, col : col + 1],
                in1=gain_sb[:, r, :].rearrange("p (u m) -> p u m", u=2),
                op0=MULT,
                op1=MULT,
            )

        def make_tables(pair, count):
            for k in range(Y_BANKS - count, Y_BANKS):
                table = work.tile([P, 2, 2, 2, 64], F32, name="table", bufs=5)
                for s in range(2):
                    for half in range(2):
                        r = 2 * k + half
                        col = (2 * pair + s) * R + r
                        nc.scalar.activation(
                            out=table[:, s, :, half, :],
                            in_=gain_sb[:, r, :].rearrange("p (u m) -> p u m", u=2),
                            func=mybir.ActivationFunctionType.Copy,
                            scale=sig[:, col : col + 1],
                        )
                tables[pair, k] = table

        def weigh_bank(pair, k, y):
            if (pair, k) in tables:
                first = 128 * (k % 2)
                nc.vector.tensor_tensor(
                    out=h_pair[pair][:, :, k // 2, :, first : first + 128].rearrange("p s u (h m) -> p s u h m", h=2),
                    in0=y[:].rearrange("p (h s u m) -> p s u h m", h=2, s=2, u=2),
                    in1=tables[pair, k][:],
                    op=MULT,
                )
            else:
                for s in range(2):
                    for half in range(2):
                        weigh_one(pair, 2 * k + half, s, y)

        def turn_h(pair, s):
            ht = bank("ht%d" % s)
            for g in range(2):
                for u in range(2):
                    col = (2 * g + u) * P
                    nc.tensor.transpose(ht[:, col : col + P], h_rows[pair, s][:, g, u, :].bitcast(F32), ident[:])
            nc.scalar.copy(
                out=staged(pair + H_LAG)[:, s * 8 * J : (s + 1) * 8 * J]
                .bitcast(F32)
                .rearrange("p (g j u) -> p g j u", g=2, u=2),
                in_=ht[:].rearrange("p (g u j) -> p g j u", g=2, u=2),
            )

        bias_sb = keep.tile([P, 2 * N], F32)
        z_banks = {}

        def second_matmul(b, tag):
            step = b // 2 + H_LAG
            z = bank(tag)
            for g in range(2):
                first = (2 * (b % 2) + g) * J
                nc.tensor.matmul_mx(
                    out=z[:],
                    lhsT=codes[step][:, first : first + J].bitcast(FP8X4),
                    lhsT_scale=scales[step][:, first : first + J],
                    rhs=c_codes[:, g, :].bitcast(FP4X4),
                    rhs_scale=c_scale_tile[:, g, :],
                    start=(g == 0),
                    stop=(g == 1),
                )
            z_banks[b] = z

        def pair_tile():
            return work.tile([P, 2 * N], F32, name="pair_tile", bufs=4)

        def over_staging(step):
            return work.tile([P, 2 * N], F32, name="summed", tag=stage_tag(step), bufs=1, align_bytes=64)

        def add_on_gpsimd(summed, copied, first, count):
            cols = slice(first, first + count)
            nc.gpsimd.tensor_tensor(out=summed[:, cols], in0=copied[:, cols], in1=bias_sb[:, cols], op=ADD)

        def add_on_vector(summed, b, first):
            base = (b % 2) * N
            nc.vector.tensor_tensor(
                out=summed[:, base + first : base + N], in0=z_banks[b][:, first:N], in1=bias_sb[:, first:N], op=ADD
            )

        def store(summed, b, count):
            base = (b % 2) * N
            nc.sync.dma_start(
                out=out[b : b + count].rearrange("b j n -> j b n"),
                in_=summed[:, base : base + count * N].rearrange("p (s n) -> p s n", s=count),
            )

        warm = bank("y0")
        for k in range(WARM_UPS):
            nc.tensor.matmul(warm[:], lhsT=zeros[:, 0:P], rhs=zeros[:], start=True, stop=True)
        turn_x(0, "ht0")
        pick = keep.tile([P, 2 * R], BF16)
        nc.vector.tensor_copy(out=pick[:], in_=ident[:, 0 : 2 * R])
        quantize(-1, 0, X_WORDS)
        spread = bank("xt")
        nc.tensor.matmul(
            spread[:, 0 : B * R], lhsT=pick[:, R : R + 1].to_broadcast([P, P]), rhs=rows[:], start=True, stop=True
        )
        nc.scalar.activation(out=sig[:], in_=spread[:, 0 : B * R], func=mybir.ActivationFunctionType.Sigmoid)
        for g, (tag, copy) in enumerate((("y2", nc.vector.tensor_copy), ("z1", nc.scalar.copy))):
            spread = bank(tag)
            for rl in range(4):
                nc.tensor.matmul(
                    spread[:, rl * I1 : (rl + 1) * I1],
                    lhsT=pick[:, 4 * g + rl : 4 * g + rl + 1].to_broadcast([P, P]),
                    rhs=rows[:, 0:I1],
                    start=True,
                    stop=True,
                )
            copy(
                out=gain_sb[:, 4 * g : 4 * g + 4, :].rearrange("p r (u q e) -> p r u q e", u=2, e=2),
                in_=spread[:].rearrange("p (r q u e) -> p r u q e", r=4, u=2, e=2),
            )

        def new_h(pair):
            h_pair[pair] = work.tile([P, 2, 2, 2, 256], BF16, name="h_pair")
            for s in range(2):
                h_rows[pair, s] = h_pair[pair][:, s, :, :, :]

        early_tags = ["z0", "y0", "y1", "y2"]
        new_h(0)
        turn_x(1, "ht1")
        ys = [first_matmul(0, k, early_tags[k]) for k in range(Y_BANKS)]
        turn_x(2, "ht0")
        turn_x(3, "ht1")
        weigh_bank(0, 0, ys[0])
        quantize(-1, X_WORDS, X_WORDS)
        for k in range(1, Y_BANKS):
            weigh_bank(0, k, ys[k])
        for step in range(1, OUT_LAG):
            new_h(step)
            ys = [first_matmul(step, k, early_tags[k]) for k in range(2)]
            make_tables(step, TABLES_BESIDE_X)
            quantize(step, 0, step_words(step))
            turn_h(step - 1, 0)
            turn_h(step - 1, 1)
            ys.extend([first_matmul(step, k, early_tags[k]) for k in range(2, Y_BANKS)])
            for k in range(Y_BANKS):
                weigh_bank(step, k, ys[k])
            if step == OUT_LAG - 2:
                for s in range(2):
                    nc.scalar.copy(out=bias_sb[:, s * N : (s + 1) * N], in_=bias_raw[:])
            turn_x(2 * step + 2, "xt")
            turn_x(2 * step + 3, "z1")

        x_ahead = OUT_LAG + 2
        last = PAIRS - 1
        for step in range(OUT_LAG, PAIRS):
            x_left = step + x_ahead < PAIRS
            done = step - OUT_LAG
            copied = pair_tile()
            for s, count in enumerate((N, GPSIMD_COLS - N)):
                second_matmul(2 * done + s, "z%d" % s)
                nc.scalar.copy(out=copied[:, s * N : s * N + count], in_=z_banks[2 * done + s][:, 0:count])
            if step < last:
                new_h(step)
                make_tables(step, TABLES_BESIDE_X if x_left else TABLES_AFTER_X)
            if step + x_ahead <= PAIRS:
                y_tags = ["y%d" % ((step - OUT_LAG + k) % 3) for k in range(3)]
                y_tags.append(y_tags[0] if x_left else "xt")
            ys = [first_matmul(step, k, y_tags[k]) for k in range(3 if x_left else Y_BANKS)]
            quantize(step, 0, step_words(step))
            summed = over_staging(step)
            add_on_gpsimd(summed, copied, 0, GPSIMD_COLS)
            if step < last:
                weigh_bank(step, 0, ys[0])
            add_on_vector(summed, 2 * done + 1, GPSIMD_COLS - N)
            store(summed, 2 * done, 2)
            if step < last:
                weigh_bank(step, 1, ys[1])
                weigh_bank(step, 2, ys[2])
                turn_h(step - 1, 0)
                turn_h(step - 1, 1)
                if x_left:
                    turn_x(step + x_ahead, "xt")
                    ys.append(first_matmul(step, 3, y_tags[3]))
                weigh_bank(step, 3, ys[3])

        for s in range(2):
            h_rows[last, s] = work.tile([P, 2, 2, 256], BF16, name="h_last", bufs=2)
            for r in range(R):
                weigh_one(last, r, s, ys[r // 2])
        turn_h(last - 1, 0)
        turn_h(last - 1, 1)
        for s in range(2):
            second_matmul(B - 6 + s, "z%d" % s)
            turn_h(last, s)
        results = [pair_tile() for k in range(3)]
        nc.scalar.copy(out=results[0][:, N : 2 * N], in_=z_banks[B - 5][:])
        quantize(last + 1, 0, H_WORDS)
        quantize(last + 2, 0, H_WORDS // 2)
        add_on_vector(results[0], B - 6, 0)
        store(results[0], B - 6, 1)
        for s in range(2):
            second_matmul(B - 4 + s, y_tags[s])
        quantize(last + 2, H_WORDS // 2, H_WORDS // 2)
        add_on_vector(results[1], B - 4, 0)
        store(results[1], B - 4, 1)
        for s in range(2):
            second_matmul(B - 2 + s, y_tags[2 + s])
        summed = over_staging(last + 2)
        add_on_gpsimd(summed, results[0], N, N)
        add_on_vector(results[1], B - 3, 0)
        store(results[1], B - 3, 1)
        add_on_vector(results[2], B - 2, 0)
        store(results[2], B - 2, 1)
        store(summed, B - 5, 1)
        add_on_vector(results[2], B - 1, 0)
        store(results[2], B - 1, 1)
